import numpy as np
import ml_dtypes


def mxq(x, axis, fmt="e4m3"):
    dtype, down = {"e4m3": (ml_dtypes.float8_e4m3fn, 7), "e5m2": (ml_dtypes.float8_e5m2, 14)}[fmt]
    v = np.moveaxis(np.asarray(x, np.float32).astype(ml_dtypes.bfloat16).astype(np.float64), axis, -1)
    blocks = v.reshape(v.shape[:-1] + (-1, 32))
    amax = np.abs(blocks).max(-1, keepdims=True)
    byte = np.maximum(np.where(amax > 0, np.frexp(amax)[1] - 1 + 127, 0) - down, 1)
    scale = np.exp2(byte - 127.0)
    codes = (blocks / scale).astype(np.float32).astype(dtype).astype(np.float64)
    return np.moveaxis((codes * scale).reshape(v.shape), -1, axis)


WIDE = False


def mx_kscale(k):
    if not WIDE:
        return np.ones(k)
    levels = np.array([10, -10, 5, -5, 0])
    if k % 512:
        return np.exp2(np.random.permutation(np.resize(levels, k // 32))).repeat(32)
    a = np.empty((k // 512, 16))
    for p in range(k // 512):
        a[p, :8] = np.random.permutation(np.resize(levels, 8))
        for g in range(8):
            far = levels[np.abs(levels - a[p, g]) >= 10]
            a[p, g + 8] = far[np.random.randint(len(far))]
    return np.exp2(a.ravel()).repeat(32)


def f64(x):
    return np.asarray(x).astype(np.float64)


def striped(idx):
    return np.tile(np.asarray(idx).reshape(-1, 16).T, (8, 1)).astype(np.uint16)


def unstriped(offs):
    return offs[:16].T.reshape(-1).astype(np.int64)


E2M1 = np.array([0.0, 0.5, 1.0, 1.5, 2.0, 3.0, 4.0, 6.0, -0.0, -0.5, -1.0, -1.5, -2.0, -3.0, -4.0, -6.0])


def pack_weight(w, fmt):
    k, n = w.shape
    w = f64(np.asarray(w, np.float32).astype(ml_dtypes.bfloat16)).reshape(k // 32, 32, n)
    amax = np.abs(w).max(1)
    if fmt == "e4m3":
        byte = np.frexp(amax)[1] - 1 + 127 - 7
    else:
        mant, ex = np.frexp(amax / 6.0)
        byte = np.where(mant > 0.5, ex, ex - 1) + 127
    byte = np.clip(np.where(amax > 0, byte, 1), 1, 254)
    scaled = (w * np.exp2(127.0 - byte)[:, None, :]).reshape(k, n).astype(np.float32)
    by_word = np.ascontiguousarray(scaled.reshape(k // 512, 128, 4, n).transpose(0, 1, 3, 2))
    if fmt == "e4m3":
        words = by_word.astype(ml_dtypes.float8_e4m3fn).view(np.uint8)
    else:
        c = by_word.astype(ml_dtypes.float4_e2m1fn).view(np.uint8) & 0xF
        words = (c[..., 0::2] | (c[..., 1::2] << 4)).reshape(k // 512, 128, 2 * n)
    return np.ascontiguousarray(words), np.ascontiguousarray(byte.astype(np.uint8).reshape(k // 512, 16, n))


def unpack_weight(words, scales, fmt):
    g, _, n = scales.shape
    words = np.ascontiguousarray(words).reshape(g, 128, n, -1)
    if fmt == "e4m3":
        vals = words.view(ml_dtypes.float8_e4m3fn).astype(np.float64)
    else:
        nib = np.empty((g, 128, n, 4), np.uint8)
        nib[..., 0::2] = words & 0xF
        nib[..., 1::2] = words >> 4
        vals = E2M1[nib]
    vals = vals * np.repeat(np.exp2(scales.astype(np.float64) - 127.0), 8, axis=1)[..., None]
    return vals.transpose(0, 1, 3, 2).reshape(g * 512, n)


D, E, T, I, Q, G = 512, 512, 2048, 512, 128, 64


def setup_inputs():
    n = np.random.standard_normal
    idx = np.random.permutation(T)[:I]
    fd = mx_kscale(D)
    fe = mx_kscale(E)
    fi = mx_kscale(I)
    ti = np.ones(T)
    ti[idx] = fi
    keysp = pack_weight(n((D, T)) / fd[:, None], "e4m3")
    valsp = pack_weight(n((E, T)) / fe[:, None], "e4m3")
    return {
        "query": (n((D, Q)) * 0.6 / np.sqrt(D) * fd[:, None]).astype(np.float32),
        "keys_words": keysp[0],
        "keys_scales": keysp[1],
        "pen": (np.random.uniform(10.0, 40.0, (Q, 1))).astype(np.float32),
        "gout": (n((E, Q)) * 1 / np.sqrt(E) * fe[:, None]).astype(np.float32),
        "vals_words": valsp[0],
        "vals_scales": valsp[1],
        "dquery": (n((D, Q)) * 1.0 / np.sqrt(D) * fd[:, None]).astype(np.float32),
        "fs": (np.random.uniform(128.0, 512.0, (1, I)) * fi).astype(np.float32),
        "keyrows": (n((D, T)) / ti).astype(np.float32),
        "res": (n((Q, D)) * 4.0).astype(np.float32),
        "offs": striped(idx),
    }


def reference(query, keys_words, keys_scales, pen, gout, vals_words, vals_scales, dquery, fs, keyrows, res, offs):
    idx = unstriped(offs)
    keysu = unpack_weight(keys_words, keys_scales, "e4m3")
    valsu = unpack_weight(vals_words, vals_scales, "e4m3")
    queryq = mxq(f64(query), 0, "e4m3")
    keysidxg = keysu[:, idx]
    a = queryq.T @ keysidxg
    dqueryq = mxq(f64(dquery), 0, "e4m3")
    ta = dqueryq.T @ keysidxg
    p = np.exp(a - np.max(a, axis=1, keepdims=True))
    z = np.sum(p, axis=1, keepdims=True)
    goutq = mxq(f64(gout), 0, "e4m3")
    valsidxg = valsu[:, idx]
    c0 = goutq.T @ valsidxg
    s = p.reshape(Q, G, I // G).sum(axis=2) / z
    ds = f64(pen) * (-1.0) * s * 2.0
    e1 = ds / z
    r1 = np.repeat(e1, I // G, axis=1)
    dz = np.sum(ds * p.reshape(Q, G, I // G).sum(axis=2) / np.square(z) * (-1.0), axis=1, keepdims=True) - np.sum(p * c0, axis=1, keepdims=True) / np.square(z)
    dp = 1.0 / z * c0 + r1 + dz
    tp = ta * p
    tz = np.sum(tp, axis=1, keepdims=True)
    ts = (tp.reshape(Q, G, I // G).sum(axis=2) - tz * p.reshape(Q, G, I // G).sum(axis=2) / z) / z
    tds = ts * f64(pen) * (-1.0) * 2.0
    te1 = (tds - tz * ds / z) / z
    tr1 = np.repeat(te1, I // G, axis=1)
    tdz = np.sum((tds * p.reshape(Q, G, I // G).sum(axis=2) + tp.reshape(Q, G, I // G).sum(axis=2) * ds - tz * z * 2.0 * ds * p.reshape(Q, G, I // G).sum(axis=2) / np.square(z)) / np.square(z) * (-1.0), axis=1, keepdims=True) - (np.sum(tp * c0, axis=1, keepdims=True) - tz * z * 2.0 * np.sum(p * c0, axis=1, keepdims=True) / np.square(z)) / np.square(z)
    tdp = tz * 1.0 / np.square(z) * (-1.0) * c0 + tr1 + tdz
    tda = tdp * p + tp * dp
    gs = tda * f64(fs)
    gt1 = gs.T
    kt = f64(keyrows)[:, idx].T
    gt1q = mxq(gt1, 0, "e4m3")
    ktq = mxq(kt, 0, "e4m3")
    gq = gt1q.T @ ktq
    y = gq + f64(res)
    return y

@@ -1,0 +1,258 @@
+from contextlib import ExitStack
+
+import concourse.mybir as mybir
+from concourse.masks import make_identity
+
+F32 = mybir.dt.float32
+BF16 = mybir.dt.bfloat16
+I32 = mybir.dt.int32
+U32 = mybir.dt.uint32
+U16 = mybir.dt.uint16
+U8 = mybir.dt.uint8
+FP8X4 = mybir.dt.float8_e4m3fn_x4
+ALU = mybir.AluOpType
+ACT = mybir.ActivationFunctionType
+AXIS = mybir.AxisListType
+
+P = 128
+PACK = 4
+D, T, I, Q, G = 512, 2048, 512, 128, 64
+BLOCKS = D // P
+VAL_PLANE = 4
+FLOPS = 4 * 2 * Q * I * D
+
+
+def tile_attend_hvcrowding_q_kernel(tc, query, keys_words, keys_scales, pen, gout, vals_words, vals_scales,
+                                     dquery, fs, keyrows, res, offs, out):
+    nc = tc.nc
+    with ExitStack() as ctx:
+        sb = ctx.enter_context(tc.tile_pool(name="sb", bufs=1))
+        ps = ctx.enter_context(tc.psum_pool(name="ps", bufs=1))
+        ps_kt = ctx.enter_context(tc.psum_pool(name="ps_kt", bufs=2))
+
+        def col(name):
+            return sb.tile([P, 1], F32, name=name)
+
+        def bank(name, tag):
+            return ps.tile([P, 512], F32, name=name, tag=tag)
+
+        def dealt(ap):
+            return ap.rearrange("p (s t) -> p t s", t=PACK)
+
+        offsets = sb.tile([P, I // 16], U16, name="offsets")
+        key_scale_pool = sb.tile([P, T], U8, name="key_scale_pool")
+        val_scale_pool = sb.tile([P, T], U8, name="val_scale_pool")
+        key_word_pool = sb.tile([P, T], U32, name="key_word_pool")
+        val_word_pool = sb.tile([P, T], U32, name="val_word_pool")
+        raw = [sb.tile([P, PACK, Q], F32, name="raw%d" % n) for n in range(3)]
+        row_pool = [sb.tile([P, T], F32, name="row_pool%d" % j, align_bytes=64) for j in range(BLOCKS)]
+        res_sb = sb.tile([P, D], F32, name="res_sb")
+        pen_sb = col("pen_sb")
+        fs_sb = sb.tile([P, PACK], F32, name="fs_sb")
+        ident = sb.tile([P, P], F32, name="ident")
+        warm_in = col("warm_in")
+        warm_out = col("warm_out")
+
+        nc.vector.memset(key_scale_pool[:].bitcast(I32), 0)
+        nc.vector.memset(val_scale_pool[:].bitcast(I32), 0)
+        nc.vector.memset(warm_in[:], 0.0)
+        nc.scalar.activation(warm_out[:], warm_in[:], ACT.Exp)
+        make_identity(nc, ident[:])
+
+        def load_words(pool, words):
+            nc.sync.dma_start(pool[:].bitcast(I32), words[0].rearrange("p n t -> p (n t)").bitcast(I32))
+
+        def load_scales(pool, scales, plane):
+            for quad in range(4):
+                first = 32 * quad + plane
+                nc.sync.dma_start(pool[first:first + 4, :].bitcast(I32),
+                                  scales[0, 4 * quad:4 * quad + 4, :].bitcast(I32))
+
+        def load_columns(dst, src):
+            nc.sync.dma_start(dst[:], src.rearrange("(p j) q -> p j q", j=PACK))
+
+        nc.sync.dma_start(offsets[:], offs)
+        load_columns(raw[0], query)
+        load_columns(raw[1], dquery)
+        load_scales(key_scale_pool, keys_scales, 0)
+        load_words(key_word_pool, keys_words)
+        load_columns(raw[2], gout)
+        load_scales(val_scale_pool, vals_scales, VAL_PLANE)
+        load_words(val_word_pool, vals_words)
+        nc.sync.dma_start(pen_sb[:], pen)
+        nc.sync.dma_start(fs_sb[:], fs[0].rearrange("(p t) -> p t", t=PACK))
+        for j in range(BLOCKS):
+            nc.sync.dma_start(row_pool[j][:], keyrows[P * j:P * (j + 1), :])
+        nc.sync.dma_start(res_sb[:], res)
+
+        def interleave(dst, src):
+            nc.scalar.copy(dst.rearrange("p (c i) t -> p c t i", i=4), src.rearrange("p t (c i) -> p c t i", i=4))
+
+        key_scales = sb.tile([P, I], U8, name="key_scales", align_bytes=64)
+        key_words = sb.tile([P, I], U32, name="key_words", align_bytes=64)
+        val_scales = sb.tile([P, I], U8, name="val_scales", align_bytes=64)
+        val_words = sb.tile([P, I], U32, name="val_words", align_bytes=64)
+        qq_bf = sb.tile([P, 2 * Q, PACK], BF16, name="qq_bf", align_bytes=64)
+        qq_codes = sb.tile([P, 2 * Q], U32, name="qq_codes", align_bytes=64)
+        qq_scales = sb.tile([P, 2 * Q], U8, name="qq_scales", align_bytes=64)
+        go_bf = sb.tile([P, Q, PACK], BF16, name="go_bf", align_bytes=64)
+        go_codes = sb.tile([P, Q], U32, name="go_codes", align_bytes=64)
+        go_scales = sb.tile([P, Q], U8, name="go_scales", align_bytes=64)
+
+        nc.vector.tensor_copy(key_scales[:], key_scale_pool[:].indirect(offsets[:]))
+        for n in range(2):
+            interleave(qq_bf[:, n * Q:(n + 1) * Q, :], raw[n][:])
+        nc.vector.quantize_mx(out=qq_codes[:].bitcast(FP8X4), scales=qq_scales[:],
+                              in_=qq_bf[:].rearrange("p q t -> p (q t)"))
+        nc.vector.tensor_copy(key_words[:], key_word_pool[:].indirect(offsets[:]))
+
+        a_ps = bank("a_ps", "bank_a")
+        ta_ps = bank("ta_ps", "bank_b")
+        for n, dst in enumerate((a_ps, ta_ps)):
+            cols = slice(n * Q, (n + 1) * Q)
+            nc.tensor.matmul_mx(out=dst[:], lhsT=qq_codes[:, cols].bitcast(FP8X4), lhsT_scale=qq_scales[:, cols],
+                                rhs=key_words[:].bitcast(FP8X4), rhs_scale=key_scales[:], start=True, stop=True)
+
+        nc.vector.tensor_copy(val_scales[:], val_scale_pool[:].indirect(offsets[:]))
+        interleave(go_bf[:], raw[2][:])
+        neg_max = sb.tile([P, 1], F32, name="neg_max", tag="val_scale_pool")
+        nc.vector.tensor_reduce(neg_max[:], a_ps[:], AXIS.X, ALU.max, negate=True)
+        nc.vector.quantize_mx(out=go_codes[:].bitcast(FP8X4), scales=go_scales[:],
+                              in_=go_bf[:].rearrange("p q t -> p (q t)"))
+        p_sb = sb.tile([P, PACK, P], F32, name="p_sb", tag="rows0")
+        z = col("z")
+        nc.scalar.activation(p_sb[:], dealt(a_ps[:]), ACT.Exp, bias=neg_max[:], accum_out=z[:])
+        nc.vector.tensor_copy(val_words[:], val_word_pool[:].indirect(offsets[:]))
+        c0_ps = bank("c0_ps", "bank_c")
+        nc.tensor.matmul_mx(out=c0_ps[:], lhsT=go_codes[:].bitcast(FP8X4), lhsT_scale=go_scales[:],
+                            rhs=val_words[:].bitcast(FP8X4), rhs_scale=val_scales[VAL_PLANE:P, :],
+                            start=True, stop=True)
+
+        rz = sb.tile([P, 1], F32, name="rz", tag="val_word_pool")
+        nc.vector.reciprocal(rz[:], z[:])
+        both = sb.tile([P, PACK, 2, P], F32, name="both")
+        w = both[:, :, 0, :]
+        wt = both[:, :, 1, :]
+        m = col("m")
+        nc.scalar.activation(w, p_sb[:], ACT.Copy, scale=rz[:])
+        nc.vector.scalar_tensor_tensor(wt, dealt(ta_ps[:]), rz[:], p_sb[:], ALU.mult, ALU.mult, accum_out=m[:])
+        wc = sb.tile([P, PACK, P], F32, name="wc", tag="rows1")
+        c_mean = col("c_mean")
+        nc.vector.scalar_tensor_tensor(wc[:], dealt(c0_ps[:]), rz[:], p_sb[:], ALU.mult, ALU.mult,
+                                       accum_out=c_mean[:])
+        term_x = sb.tile([P, PACK, P], F32, name="term_x")
+        x_sum = col("x_sum")
+        nc.vector.scalar_tensor_tensor(term_x[:], dealt(ta_ps[:]), m[:], wc[:], ALU.subtract, ALU.mult,
+                                       accum_out=x_sum[:])
+
+        pages_t = bank("pages_t", "bank_f")
+        both_flat = both[:].rearrange("p t a s -> p t (a s)")
+        for t in range(PACK):
+            for e in range(2):
+                nc.tensor.matmul(pages_t[:, 0:Q], lhsT=both_flat[:, t, e:2 * P:2], rhs=ident[:], is_transpose=True,
+                                 start=(t == 0 and e == 0), stop=(t == PACK - 1 and e == 1))
+        pages_t_sb = sb.tile([P, Q], F32, name="pages_t_sb")
+        nc.scalar.copy(pages_t_sb[:], pages_t[:, 0:Q])
+        pages = bank("pages", "bank_a")
+        nc.tensor.transpose(pages[:, 0:P], pages_t_sb[:], ident[:])
+        share = pages[:, 0:G]
+        tshare = pages[:, G:2 * G]
+
+        c2 = col("c2")
+        m2 = col("m2")
+        m3c2 = col("m3c2")
+        c6 = col("c6")
+        mc = col("mc")
+        e0 = col("e0")
+        nc.scalar.activation(c2[:], pen_sb[:], ACT.Copy, scale=-2.0)
+        nc.scalar.activation(c6[:], pen_sb[:], ACT.Copy, scale=-6.0)
+        nc.scalar.activation(m2[:], m[:], ACT.Copy, scale=-2.0)
+        nc.scalar.activation(m3c2[:], m[:], ACT.Copy, scale=c6[:])
+        nc.scalar.activation(mc[:], c_mean[:], ACT.Copy, scale=m[:])
+        nc.scalar.activation(e0[:], x_sum[:], ACT.Identity, scale=-1.0, bias=mc[:])
+
+        gt_ps = [bank("gt%d" % t, tag) for t, tag in enumerate(("bank_b", "bank_c", "bank_d", "bank_e"))]
+
+        def turn_term(term, start, stop):
+            for t in range(PACK):
+                nc.tensor.matmul(gt_ps[t][:, 0:Q], lhsT=term[:, t, :], rhs=ident[:], is_transpose=True,
+                                 start=start, stop=stop)
+
+        turn_term(term_x, True, False)
+
+        kt_scales = sb.tile([P, D], U8, name="kt_scales", align_bytes=64)
+        kt_bf = sb.tile([P, D, PACK], BF16, name="kt_bf", align_bytes=64)
+
+        def gather_rows(j):
+            rows = sb.tile([P, I], BF16, name="rows%d" % j)
+            nc.vector.tensor_copy(rows[:], row_pool[j][:].indirect(offsets[:]))
+            words = rows[:].bitcast(F32)
+            turned = ps_kt.tile([P, 2, P], F32, name="turned")
+            for u in range(2):
+                nc.tensor.transpose(turned[:, u, :], words[:, u:I // 2:2], ident[:])
+            nc.scalar.copy(kt_bf[:, P * j:P * (j + 1), :].bitcast(F32), turned[:].rearrange("p u d -> p d u"))
+
+        def quantise_rows(codes, cols):
+            nc.vector.quantize_mx(out=codes.bitcast(FP8X4), scales=kt_scales[:, cols],
+                                  in_=kt_bf[:, cols, :].rearrange("p d t -> p (d t)"))
+
+        gather_rows(0)
+        gather_rows(1)
+
+        ds2 = sb.tile([P, G, 2], F32, name="ds2")
+        tc2 = sb.tile([P, G, 2], F32, name="tc2")
+        squares = sb.tile([P, G], F32, name="squares")
+        s2 = col("s2")
+        ac = col("ac")
+        nc.scalar.activation(ds2[:], share.unsqueeze(2).to_broadcast([P, G, 2]), ACT.Copy, scale=c2[:])
+        nc.scalar.activation(tc2[:], tshare.unsqueeze(2).to_broadcast([P, G, 2]), ACT.Identity, scale=c2[:],
+                             bias=e0[:])
+        nc.scalar.activation(squares[:], share, ACT.Square, accum_out=s2[:])
+        nc.scalar.activation(ac[:], s2[:], ACT.Identity, scale=c2[:], bias=c_mean[:])
+        cross = sb.tile([P, G], F32, name="cross")
+        b_sum = col("b_sum")
+        kappa = col("kappa")
+        r2 = sb.tile([P, P], F32, name="r2", tag="rows2")
+        ds_flat = ds2[:].rearrange("p g e -> p (g e)")
+        nc.vector.scalar_tensor_tensor(cross[:], tshare, -2.0, ds2[:, :, 0], ALU.mult, ALU.mult, accum_out=b_sum[:])
+        nc.vector.scalar_tensor_tensor(r2[:], ds_flat, m2[:], tc2[:].rearrange("p g e -> p (g e)"), ALU.mult, ALU.add)
+        nc.scalar.activation(kappa[:], s2[:], ACT.Identity, scale=m3c2[:], bias=b_sum[:])
+        term_d = sb.tile([P, PACK, P], F32, name="term_d")
+        term_f = sb.tile([P, PACK, P], F32, name="term_f")
+        nc.vector.scalar_tensor_tensor(term_d[:], ds_flat.unsqueeze(1).to_broadcast([P, PACK, P]), ac[:], wt,
+                                       ALU.subtract, ALU.mult)
+        turn_term(term_d, False, False)
+        nc.vector.scalar_tensor_tensor(term_f[:], r2[:].unsqueeze(1).to_broadcast([P, PACK, P]), kappa[:], w,
+                                       ALU.add, ALU.mult)
+        turn_term(term_f, False, True)
+        gt_bf = sb.tile([P, Q, PACK], BF16, name="gt_bf", align_bytes=64)
+        gt_scales = sb.tile([P, Q], U8, name="gt_scales", align_bytes=64)
+        gt_planes = sb.tile([P, PACK, Q], BF16, name="gt_planes")
+        for t in range(PACK):
+            nc.scalar.activation(gt_planes[:, t, :], gt_ps[t][:, 0:Q], ACT.Copy, scale=fs_sb[:, t:t + 1])
+        interleave(gt_bf[:], gt_planes[:])
+        gather_rows(2)
+        codes01 = sb.tile([P, 2 * P], U32, name="codes01", tag="row_pool2", align_bytes=64)
+        quantise_rows(codes01[:], slice(0, 2 * P))
+        gather_rows(3)
+        late_codes = sb.tile([P, 2 * P], U32, name="late_codes", tag="row_pool3", align_bytes=64)
+        codes3 = sb.tile([P, P], U32, name="codes3", align_bytes=64)
+        gt_codes = late_codes[:, P:2 * P]
+        quantise_rows(late_codes[:, 0:P], slice(2 * P, 3 * P))
+        nc.vector.quantize_mx(out=gt_codes.bitcast(FP8X4), scales=gt_scales[:],
+                              in_=gt_bf[:].rearrange("p q t -> p (q t)"))
+        quantise_rows(codes3[:], slice(3 * P, D))
+
+        early = (BLOCKS - 1) * P
+        out_early = bank("out_early", "bank_d")
+        out_last = bank("out_last", "bank_e")
+        out_sb = sb.tile([P, D], F32, name="out_sb")
+        for dst, codes, cols in ((out_early[:, 0:2 * P], codes01[:], slice(0, 2 * P)),
+                                 (out_early[:, 2 * P:early], late_codes[:, 0:P], slice(2 * P, early)),
+                                 (out_last[:, 0:P], codes3[:], slice(early, D))):
+            nc.tensor.matmul_mx(out=dst, lhsT=gt_codes.bitcast(FP8X4), lhsT_scale=gt_scales[:],
+                                rhs=codes.bitcast(FP8X4), rhs_scale=kt_scales[:, cols], start=True, stop=True)
+        nc.vector.tensor_tensor(out_sb[:, 0:early], out_early[:, 0:early], res_sb[:, 0:early], ALU.add)
+        nc.sync.dma_start(out[:, 0:early], out_sb[:, 0:early])
+        nc.vector.tensor_tensor(out_sb[:, early:D], out_last[:, 0:P], res_sb[:, early:D], ALU.add)
+        nc.sync.dma_start(out[:, early:D], out_sb[:, early:D])

@@ -28,7 +28,6 @@ def tile_attend_hvcrowding_q_kernel(tc, query, keys_words, keys_scales, pen, gou
     with ExitStack() as ctx:
         sb = ctx.enter_context(tc.tile_pool(name="sb", bufs=1))
         ps = ctx.enter_context(tc.psum_pool(name="ps", bufs=1))
-        ps_kt = ctx.enter_context(tc.psum_pool(name="ps_kt", bufs=2))
 
         def col(name):
             return sb.tile([P, 1], F32, name=name)
@@ -59,8 +58,8 @@ def tile_attend_hvcrowding_q_kernel(tc, query, keys_words, keys_scales, pen, gou
         nc.scalar.activation(warm_out[:], warm_in[:], ACT.Exp)
         make_identity(nc, ident[:])
 
-        def load_words(pool, words):
-            nc.sync.dma_start(pool[:].bitcast(I32), words[0].rearrange("p n t -> p (n t)").bitcast(I32))
+        def load_words(pool, words, cols):
+            nc.sync.dma_start(pool[:, cols].bitcast(I32), words[0, :, cols, :].rearrange("p n t -> p (n t)").bitcast(I32))
 
         def load_scales(pool, scales, plane):
             for quad in range(4):
@@ -74,11 +73,12 @@ def tile_attend_hvcrowding_q_kernel(tc, query, keys_words, keys_scales, pen, gou
         nc.sync.dma_start(offsets[:], offs)
         load_columns(raw[0], query)
         load_columns(raw[1], dquery)
+        load_words(key_word_pool, keys_words, slice(0, 3 * T // 4))
         load_scales(key_scale_pool, keys_scales, 0)
-        load_words(key_word_pool, keys_words)
+        load_words(key_word_pool, keys_words, slice(3 * T // 4, T))
         load_columns(raw[2], gout)
         load_scales(val_scale_pool, vals_scales, VAL_PLANE)
-        load_words(val_word_pool, vals_words)
+        load_words(val_word_pool, vals_words, slice(0, T))
         nc.sync.dma_start(pen_sb[:], pen)
         nc.sync.dma_start(fs_sb[:], fs[0].rearrange("(p t) -> p t", t=PACK))
         for j in range(BLOCKS):
@@ -180,24 +180,21 @@ def tile_attend_hvcrowding_q_kernel(tc, query, keys_words, keys_scales, pen, gou
 
         turn_term(term_x, True, False)
 
-        kt_scales = sb.tile([P, D], U8, name="kt_scales", align_bytes=64)
-        kt_bf = sb.tile([P, D, PACK], BF16, name="kt_bf", align_bytes=64)
+        early = (BLOCKS - 1) * P
+        early_bf = sb.tile([P, early + Q, PACK], BF16, name="early_bf", align_bytes=64)
+        last_bf = sb.tile([P, P, PACK], BF16, name="last_bf", align_bytes=64)
+        kt_bf = [early_bf[:, P * j:P * (j + 1), :] for j in range(BLOCKS - 1)] + [last_bf[:]]
+        gt_bf = early_bf[:, early:early + Q, :]
 
         def gather_rows(j):
             rows = sb.tile([P, I], BF16, name="rows%d" % j)
             nc.vector.tensor_copy(rows[:], row_pool[j][:].indirect(offsets[:]))
             words = rows[:].bitcast(F32)
-            turned = ps_kt.tile([P, 2, P], F32, name="turned")
+            turned = ps.tile([P, 2, P], F32, name="turned%d" % j, tag=("bank_f", "bank_g", "bank_h", "bank_g")[j])
             for u in range(2):
                 nc.tensor.transpose(turned[:, u, :], words[:, u:I // 2:2], ident[:])
-            nc.scalar.copy(kt_bf[:, P * j:P * (j + 1), :].bitcast(F32), turned[:].rearrange("p u d -> p d u"))
+            nc.scalar.copy(kt_bf[j].bitcast(F32), turned[:].rearrange("p u d -> p d u"))
 
-        def quantise_rows(codes, cols):
-            nc.vector.quantize_mx(out=codes.bitcast(FP8X4), scales=kt_scales[:, cols],
-                                  in_=kt_bf[:, cols, :].rearrange("p d t -> p (d t)"))
-
-        gather_rows(0)
-        gather_rows(1)
 
         ds2 = sb.tile([P, G, 2], F32, name="ds2")
         tc2 = sb.tile([P, G, 2], F32, name="tc2")
@@ -209,49 +206,49 @@ def tile_attend_hvcrowding_q_kernel(tc, query, keys_words, keys_scales, pen, gou
                              bias=e0[:])
         nc.scalar.activation(squares[:], share, ACT.Square, accum_out=s2[:])
         nc.scalar.activation(ac[:], s2[:], ACT.Identity, scale=c2[:], bias=c_mean[:])
-        cross = sb.tile([P, G], F32, name="cross")
+        gather_rows(0)
+        gather_rows(1)
+        late = sb.tile([P, 2 * I + 2 * P], F32, name="late", tag="row_pool1", align_bytes=64)
+        term_d = late[:, 0:I].rearrange("p (t s) -> p t s", t=PACK)
+        term_f = late[:, I:2 * I].rearrange("p (t s) -> p t s", t=PACK)
+        r2 = late[:, 2 * I:2 * I + P]
+        cross = late[:, 2 * I + P:2 * I + P + G]
         b_sum = col("b_sum")
-        kappa = col("kappa")
-        r2 = sb.tile([P, P], F32, name="r2", tag="rows2")
+        kappa = sb.tile([P, 1], F32, name="kappa", tag="rows2")
         ds_flat = ds2[:].rearrange("p g e -> p (g e)")
-        nc.vector.scalar_tensor_tensor(cross[:], tshare, -2.0, ds2[:, :, 0], ALU.mult, ALU.mult, accum_out=b_sum[:])
-        nc.vector.scalar_tensor_tensor(r2[:], ds_flat, m2[:], tc2[:].rearrange("p g e -> p (g e)"), ALU.mult, ALU.add)
+        nc.vector.scalar_tensor_tensor(cross, tshare, -2.0, ds2[:, :, 0], ALU.mult, ALU.mult, accum_out=b_sum[:])
+        nc.vector.scalar_tensor_tensor(r2, ds_flat, m2[:], tc2[:].rearrange("p g e -> p (g e)"), ALU.mult, ALU.add)
         nc.scalar.activation(kappa[:], s2[:], ACT.Identity, scale=m3c2[:], bias=b_sum[:])
-        term_d = sb.tile([P, PACK, P], F32, name="term_d")
-        term_f = sb.tile([P, PACK, P], F32, name="term_f")
-        nc.vector.scalar_tensor_tensor(term_d[:], ds_flat.unsqueeze(1).to_broadcast([P, PACK, P]), ac[:], wt,
+        nc.vector.scalar_tensor_tensor(term_d, ds_flat.unsqueeze(1).to_broadcast([P, PACK, P]), ac[:], wt,
                                        ALU.subtract, ALU.mult)
         turn_term(term_d, False, False)
-        nc.vector.scalar_tensor_tensor(term_f[:], r2[:].unsqueeze(1).to_broadcast([P, PACK, P]), kappa[:], w,
+        nc.vector.scalar_tensor_tensor(term_f, r2.unsqueeze(1).to_broadcast([P, PACK, P]), kappa[:], w,
                                        ALU.add, ALU.mult)
         turn_term(term_f, False, True)
-        gt_bf = sb.tile([P, Q, PACK], BF16, name="gt_bf", align_bytes=64)
-        gt_scales = sb.tile([P, Q], U8, name="gt_scales", align_bytes=64)
         gt_planes = sb.tile([P, PACK, Q], BF16, name="gt_planes")
         for t in range(PACK):
             nc.scalar.activation(gt_planes[:, t, :], gt_ps[t][:, 0:Q], ACT.Copy, scale=fs_sb[:, t:t + 1])
-        interleave(gt_bf[:], gt_planes[:])
+        interleave(gt_bf, gt_planes[:])
         gather_rows(2)
-        codes01 = sb.tile([P, 2 * P], U32, name="codes01", tag="row_pool2", align_bytes=64)
-        quantise_rows(codes01[:], slice(0, 2 * P))
         gather_rows(3)
-        late_codes = sb.tile([P, 2 * P], U32, name="late_codes", tag="row_pool3", align_bytes=64)
-        codes3 = sb.tile([P, P], U32, name="codes3", align_bytes=64)
-        gt_codes = late_codes[:, P:2 * P]
-        quantise_rows(late_codes[:, 0:P], slice(2 * P, 3 * P))
-        nc.vector.quantize_mx(out=gt_codes.bitcast(FP8X4), scales=gt_scales[:],
-                              in_=gt_bf[:].rearrange("p q t -> p (q t)"))
-        quantise_rows(codes3[:], slice(3 * P, D))
+        early_codes = sb.tile([P, early + Q], U32, name="early_codes", tag="row_pool3", align_bytes=64)
+        early_scales = sb.tile([P, early + Q], U8, name="early_scales", align_bytes=64)
+        last_codes = sb.tile([P, P], U32, name="last_codes", align_bytes=64)
+        last_scales = sb.tile([P, P], U8, name="last_scales", align_bytes=64)
+        nc.vector.quantize_mx(out=early_codes[:].bitcast(FP8X4), scales=early_scales[:],
+                              in_=early_bf[:].rearrange("p d t -> p (d t)"))
+        nc.vector.quantize_mx(out=last_codes[:].bitcast(FP8X4), scales=last_scales[:],
+                              in_=last_bf[:].rearrange("p d t -> p (d t)"))
 
-        early = (BLOCKS - 1) * P
         out_early = bank("out_early", "bank_d")
         out_last = bank("out_last", "bank_e")
         out_sb = sb.tile([P, D], F32, name="out_sb")
-        for dst, codes, cols in ((out_early[:, 0:2 * P], codes01[:], slice(0, 2 * P)),
-                                 (out_early[:, 2 * P:early], late_codes[:, 0:P], slice(2 * P, early)),
-                                 (out_last[:, 0:P], codes3[:], slice(early, D))):
-            nc.tensor.matmul_mx(out=dst, lhsT=gt_codes.bitcast(FP8X4), lhsT_scale=gt_scales[:],
-                                rhs=codes.bitcast(FP8X4), rhs_scale=kt_scales[:, cols], start=True, stop=True)
+        gt_cols = slice(early, early + Q)
+        for dst, codes, scales in ((out_early[:, 0:2 * P], early_codes[:, 0:2 * P], early_scales[:, 0:2 * P]),
+                                   (out_early[:, 2 * P:early], early_codes[:, 2 * P:early], early_scales[:, 2 * P:early]),
+                                   (out_last[:, 0:P], last_codes[:], last_scales[:])):
+            nc.tensor.matmul_mx(out=dst, lhsT=early_codes[:, gt_cols].bitcast(FP8X4), lhsT_scale=early_scales[:, gt_cols],
+                                rhs=codes.bitcast(FP8X4), rhs_scale=scales, start=True, stop=True)
         nc.vector.tensor_tensor(out_sb[:, 0:early], out_early[:, 0:early], res_sb[:, 0:early], ALU.add)
         nc.sync.dma_start(out[:, 0:early], out_sb[:, 0:early])
         nc.vector.tensor_tensor(out_sb[:, early:D], out_last[:, 0:P], res_sb[:, early:D], ALU.add)

@@ -71,17 +71,18 @@ def tile_attend_hvcrowding_q_kernel(tc, query, keys_words, keys_scales, pen, gou
             nc.sync.dma_start(dst[:], src.rearrange("(p j) q -> p j q", j=PACK))
 
         nc.sync.dma_start(offsets[:], offs)
+        load_words(key_word_pool, keys_words, slice(0, T // 2))
+        load_scales(key_scale_pool, keys_scales, 0)
+        load_words(key_word_pool, keys_words, slice(T // 2, T))
         load_columns(raw[0], query)
         load_columns(raw[1], dquery)
-        load_words(key_word_pool, keys_words, slice(0, 3 * T // 4))
-        load_scales(key_scale_pool, keys_scales, 0)
-        load_words(key_word_pool, keys_words, slice(3 * T // 4, T))
         load_columns(raw[2], gout)
         load_scales(val_scale_pool, vals_scales, VAL_PLANE)
         load_words(val_word_pool, vals_words, slice(0, T))
+        nc.sync.dma_start(row_pool[0][:], keyrows[0:P, :])
         nc.sync.dma_start(pen_sb[:], pen)
         nc.sync.dma_start(fs_sb[:], fs[0].rearrange("(p t) -> p t", t=PACK))
-        for j in range(BLOCKS):
+        for j in range(1, BLOCKS):
             nc.sync.dma_start(row_pool[j][:], keyrows[P * j:P * (j + 1), :])
         nc.sync.dma_start(res_sb[:], res)
 
@@ -100,11 +101,12 @@ def tile_attend_hvcrowding_q_kernel(tc, query, keys_words, keys_scales, pen, gou
         go_scales = sb.tile([P, Q], U8, name="go_scales", align_bytes=64)
 
         nc.vector.tensor_copy(key_scales[:], key_scale_pool[:].indirect(offsets[:]))
-        for n in range(2):
-            interleave(qq_bf[:, n * Q:(n + 1) * Q, :], raw[n][:])
-        nc.vector.quantize_mx(out=qq_codes[:].bitcast(FP8X4), scales=qq_scales[:],
-                              in_=qq_bf[:].rearrange("p q t -> p (q t)"))
         nc.vector.tensor_copy(key_words[:], key_word_pool[:].indirect(offsets[:]))
+        for n in range(2):
+            cols = slice(n * Q, (n + 1) * Q)
+            interleave(qq_bf[:, cols, :], raw[n][:])
+            nc.vector.quantize_mx(out=qq_codes[:, cols].bitcast(FP8X4), scales=qq_scales[:, cols],
+                                  in_=qq_bf[:, cols, :].rearrange("p q t -> p (q t)"))
 
         a_ps = bank("a_ps", "bank_a")
         ta_ps = bank("ta_ps", "bank_b")
@@ -164,8 +166,8 @@ def tile_attend_hvcrowding_q_kernel(tc, query, keys_words, keys_scales, pen, gou
         c6 = col("c6")
         mc = col("mc")
         e0 = col("e0")
-        nc.scalar.activation(c2[:], pen_sb[:], ACT.Copy, scale=-2.0)
-        nc.scalar.activation(c6[:], pen_sb[:], ACT.Copy, scale=-6.0)
+        nc.gpsimd.tensor_scalar(c2[:], pen_sb[:], -2.0, None, ALU.mult)
+        nc.gpsimd.tensor_scalar(c6[:], pen_sb[:], -6.0, None, ALU.mult)
         nc.scalar.activation(m2[:], m[:], ACT.Copy, scale=-2.0)
         nc.scalar.activation(m3c2[:], m[:], ACT.Copy, scale=c6[:])
         nc.scalar.activation(mc[:], c_mean[:], ACT.Copy, scale=m[:])

from contextlib import ExitStack

import concourse.mybir as mybir
from concourse.masks import make_identity

F32 = mybir.dt.float32
BF16 = mybir.dt.bfloat16
I32 = mybir.dt.int32
U32 = mybir.dt.uint32
U16 = mybir.dt.uint16
U8 = mybir.dt.uint8
FP8X4 = mybir.dt.float8_e4m3fn_x4
ALU = mybir.AluOpType
ACT = mybir.ActivationFunctionType
AXIS = mybir.AxisListType

P = 128
PACK = 4
D, T, I, Q, G = 512, 2048, 512, 128, 64
BLOCKS = D // P
VAL_PLANE = 4
FLOPS = 4 * 2 * Q * I * D


def tile_attend_hvcrowding_q_kernel(tc, query, keys_words, keys_scales, pen, gout, vals_words, vals_scales,
                                     dquery, fs, keyrows, res, offs, out):
    nc = tc.nc
    with ExitStack() as ctx:
        sb = ctx.enter_context(tc.tile_pool(name="sb", bufs=1))
        ps = ctx.enter_context(tc.psum_pool(name="ps", bufs=1))

        def col(name):
            return sb.tile([P, 1], F32, name=name)

        def bank(name, tag):
            return ps.tile([P, 512], F32, name=name, tag=tag)

        def dealt(ap):
            return ap.rearrange("p (s t) -> p t s", t=PACK)

        offsets = sb.tile([P, I // 16], U16, name="offsets")
        key_scale_pool = sb.tile([P, T], U8, name="key_scale_pool")
        val_scale_pool = sb.tile([P, T], U8, name="val_scale_pool")
        key_word_pool = sb.tile([P, T], U32, name="key_word_pool")
        val_word_pool = sb.tile([P, T], U32, name="val_word_pool")
        raw = [sb.tile([P, PACK, Q], F32, name="raw%d" % n) for n in range(3)]
        row_pool = [sb.tile([P, T], F32, name="row_pool%d" % j, align_bytes=64) for j in range(BLOCKS)]
        res_sb = sb.tile([P, D], F32, name="res_sb")
        pen_sb = col("pen_sb")
        fs_sb = sb.tile([P, PACK], F32, name="fs_sb")
        ident = sb.tile([P, P], F32, name="ident")
        warm_in = col("warm_in")
        warm_out = col("warm_out")

        nc.vector.memset(key_scale_pool[:].bitcast(I32), 0)
        nc.vector.memset(val_scale_pool[:].bitcast(I32), 0)
        nc.vector.memset(warm_in[:], 0.0)
        nc.scalar.activation(warm_out[:], warm_in[:], ACT.Exp)
        make_identity(nc, ident[:])

        def load_words(pool, words, cols):
            nc.sync.dma_start(pool[:, cols].bitcast(I32), words[0, :, cols, :].rearrange("p n t -> p (n t)").bitcast(I32))

        def load_scales(pool, scales, plane):
            for quad in range(4):
                first = 32 * quad + plane
                nc.sync.dma_start(pool[first:first + 4, :].bitcast(I32),
                                  scales[0, 4 * quad:4 * quad + 4, :].bitcast(I32))

        def load_columns(dst, src):
            nc.sync.dma_start(dst[:], src.rearrange("(p j) q -> p j q", j=PACK))

        nc.sync.dma_start(offsets[:], offs)
        load_words(key_word_pool, keys_words, slice(0, T // 2))
        load_scales(key_scale_pool, keys_scales, 0)
        load_words(key_word_pool, keys_words, slice(T // 2, T))
        load_columns(raw[0], query)
        load_columns(raw[1], dquery)
        load_columns(raw[2], gout)
        load_scales(val_scale_pool, vals_scales, VAL_PLANE)
        load_words(val_word_pool, vals_words, slice(0, T))
        nc.sync.dma_start(row_pool[0][:], keyrows[0:P, :])
        nc.sync.dma_start(pen_sb[:], pen)
        nc.sync.dma_start(fs_sb[:], fs[0].rearrange("(p t) -> p t", t=PACK))
        for j in range(1, BLOCKS):
            nc.sync.dma_start(row_pool[j][:], keyrows[P * j:P * (j + 1), :])
        nc.sync.dma_start(res_sb[:], res)

        def interleave(dst, src):
            nc.scalar.copy(dst.rearrange("p (c i) t -> p c t i", i=4), src.rearrange("p t (c i) -> p c t i", i=4))

        key_scales = sb.tile([P, I], U8, name="key_scales", align_bytes=64)
        key_words = sb.tile([P, I], U32, name="key_words", align_bytes=64)
        val_scales = sb.tile([P, I], U8, name="val_scales", align_bytes=64)
        val_words = sb.tile([P, I], U32, name="val_words", align_bytes=64)
        qq_bf = sb.tile([P, 2 * Q, PACK], BF16, name="qq_bf", align_bytes=64)
        qq_codes = sb.tile([P, 2 * Q], U32, name="qq_codes", align_bytes=64)
        qq_scales = sb.tile([P, 2 * Q], U8, name="qq_scales", align_bytes=64)
        go_bf = sb.tile([P, Q, PACK], BF16, name="go_bf", align_bytes=64)
        go_codes = sb.tile([P, Q], U32, name="go_codes", align_bytes=64)
        go_scales = sb.tile([P, Q], U8, name="go_scales", align_bytes=64)

        nc.vector.tensor_copy(key_scales[:], key_scale_pool[:].indirect(offsets[:]))
        nc.vector.tensor_copy(key_words[:], key_word_pool[:].indirect(offsets[:]))
        for n in range(2):
            cols = slice(n * Q, (n + 1) * Q)
            interleave(qq_bf[:, cols, :], raw[n][:])
            nc.vector.quantize_mx(out=qq_codes[:, cols].bitcast(FP8X4), scales=qq_scales[:, cols],
                                  in_=qq_bf[:, cols, :].rearrange("p q t -> p (q t)"))

        a_ps = bank("a_ps", "bank_a")
        ta_ps = bank("ta_ps", "bank_b")
        for n, dst in enumerate((a_ps, ta_ps)):
            cols = slice(n * Q, (n + 1) * Q)
            nc.tensor.matmul_mx(out=dst[:], lhsT=qq_codes[:, cols].bitcast(FP8X4), lhsT_scale=qq_scales[:, cols],
                                rhs=key_words[:].bitcast(FP8X4), rhs_scale=key_scales[:], start=True, stop=True)

        nc.vector.tensor_copy(val_scales[:], val_scale_pool[:].indirect(offsets[:]))
        interleave(go_bf[:], raw[2][:])
        neg_max = sb.tile([P, 1], F32, name="neg_max", tag="val_scale_pool")
        nc.vector.tensor_reduce(neg_max[:], a_ps[:], AXIS.X, ALU.max, negate=True)
        nc.vector.quantize_mx(out=go_codes[:].bitcast(FP8X4), scales=go_scales[:],
                              in_=go_bf[:].rearrange("p q t -> p (q t)"))
        p_sb = sb.tile([P, PACK, P], F32, name="p_sb", tag="rows0")
        z = col("z")
        nc.scalar.activation(p_sb[:], dealt(a_ps[:]), ACT.Exp, bias=neg_max[:], accum_out=z[:])
        nc.vector.tensor_copy(val_words[:], val_word_pool[:].indirect(offsets[:]))
        c0_ps = bank("c0_ps", "bank_c")
        nc.tensor.matmul_mx(out=c0_ps[:], lhsT=go_codes[:].bitcast(FP8X4), lhsT_scale=go_scales[:],
                            rhs=val_words[:].bitcast(FP8X4), rhs_scale=val_scales[VAL_PLANE:P, :],
                            start=True, stop=True)

        rz = sb.tile([P, 1], F32, name="rz", tag="val_word_pool")
        nc.vector.reciprocal(rz[:], z[:])
        both = sb.tile([P, PACK, 2, P], F32, name="both")
        w = both[:, :, 0, :]
        wt = both[:, :, 1, :]
        m = col("m")
        nc.scalar.activation(w, p_sb[:], ACT.Copy, scale=rz[:])
        nc.vector.scalar_tensor_tensor(wt, dealt(ta_ps[:]), rz[:], p_sb[:], ALU.mult, ALU.mult, accum_out=m[:])
        wc = sb.tile([P, PACK, P], F32, name="wc", tag="rows1")
        c_mean = col("c_mean")
        nc.vector.scalar_tensor_tensor(wc[:], dealt(c0_ps[:]), rz[:], p_sb[:], ALU.mult, ALU.mult,
                                       accum_out=c_mean[:])
        term_x = sb.tile([P, PACK, P], F32, name="term_x")
        x_sum = col("x_sum")
        nc.vector.scalar_tensor_tensor(term_x[:], dealt(ta_ps[:]), m[:], wc[:], ALU.subtract, ALU.mult,
                                       accum_out=x_sum[:])

        pages_t = bank("pages_t", "bank_f")
        both_flat = both[:].rearrange("p t a s -> p t (a s)")
        for t in range(PACK):
            for e in range(2):
                nc.tensor.matmul(pages_t[:, 0:Q], lhsT=both_flat[:, t, e:2 * P:2], rhs=ident[:], is_transpose=True,
                                 start=(t == 0 and e == 0), stop=(t == PACK - 1 and e == 1))
        pages_t_sb = sb.tile([P, Q], F32, name="pages_t_sb")
        nc.scalar.copy(pages_t_sb[:], pages_t[:, 0:Q])
        pages = bank("pages", "bank_a")
        nc.tensor.transpose(pages[:, 0:P], pages_t_sb[:], ident[:])
        share = pages[:, 0:G]
        tshare = pages[:, G:2 * G]

        c2 = col("c2")
        m2 = col("m2")
        m3c2 = col("m3c2")
        c6 = col("c6")
        mc = col("mc")
        e0 = col("e0")
        nc.gpsimd.tensor_scalar(c2[:], pen_sb[:], -2.0, None, ALU.mult)
        nc.gpsimd.tensor_scalar(c6[:], pen_sb[:], -6.0, None, ALU.mult)
        nc.scalar.activation(m2[:], m[:], ACT.Copy, scale=-2.0)
        nc.scalar.activation(m3c2[:], m[:], ACT.Copy, scale=c6[:])
        nc.scalar.activation(mc[:], c_mean[:], ACT.Copy, scale=m[:])
        nc.scalar.activation(e0[:], x_sum[:], ACT.Identity, scale=-1.0, bias=mc[:])

        gt_ps = [bank("gt%d" % t, tag) for t, tag in enumerate(("bank_b", "bank_c", "bank_d", "bank_e"))]

        def turn_term(term, start, stop):
            for t in range(PACK):
                nc.tensor.matmul(gt_ps[t][:, 0:Q], lhsT=term[:, t, :], rhs=ident[:], is_transpose=True,
                                 start=start, stop=stop)

        turn_term(term_x, True, False)

        early = (BLOCKS - 1) * P
        early_bf = sb.tile([P, early + Q, PACK], BF16, name="early_bf", align_bytes=64)
        last_bf = sb.tile([P, P, PACK], BF16, name="last_bf", align_bytes=64)
        kt_bf = [early_bf[:, P * j:P * (j + 1), :] for j in range(BLOCKS - 1)] + [last_bf[:]]
        gt_bf = early_bf[:, early:early + Q, :]

        def gather_rows(j):
            rows = sb.tile([P, I], BF16, name="rows%d" % j)
            nc.vector.tensor_copy(rows[:], row_pool[j][:].indirect(offsets[:]))
            words = rows[:].bitcast(F32)
            turned = ps.tile([P, 2, P], F32, name="turned%d" % j, tag=("bank_f", "bank_g", "bank_h", "bank_g")[j])
            for u in range(2):
                nc.tensor.transpose(turned[:, u, :], words[:, u:I // 2:2], ident[:])
            nc.scalar.copy(kt_bf[j].bitcast(F32), turned[:].rearrange("p u d -> p d u"))


        ds2 = sb.tile([P, G, 2], F32, name="ds2")
        tc2 = sb.tile([P, G, 2], F32, name="tc2")
        squares = sb.tile([P, G], F32, name="squares")
        s2 = col("s2")
        ac = col("ac")
        nc.scalar.activation(ds2[:], share.unsqueeze(2).to_broadcast([P, G, 2]), ACT.Copy, scale=c2[:])
        nc.scalar.activation(tc2[:], tshare.unsqueeze(2).to_broadcast([P, G, 2]), ACT.Identity, scale=c2[:],
                             bias=e0[:])
        nc.scalar.activation(squares[:], share, ACT.Square, accum_out=s2[:])
        nc.scalar.activation(ac[:], s2[:], ACT.Identity, scale=c2[:], bias=c_mean[:])
        gather_rows(0)
        gather_rows(1)
        late = sb.tile([P, 2 * I + 2 * P], F32, name="late", tag="row_pool1", align_bytes=64)
        term_d = late[:, 0:I].rearrange("p (t s) -> p t s", t=PACK)
        term_f = late[:, I:2 * I].rearrange("p (t s) -> p t s", t=PACK)
        r2 = late[:, 2 * I:2 * I + P]
        cross = late[:, 2 * I + P:2 * I + P + G]
        b_sum = col("b_sum")
        kappa = sb.tile([P, 1], F32, name="kappa", tag="rows2")
        ds_flat = ds2[:].rearrange("p g e -> p (g e)")
        nc.vector.scalar_tensor_tensor(cross, tshare, -2.0, ds2[:, :, 0], ALU.mult, ALU.mult, accum_out=b_sum[:])
        nc.vector.scalar_tensor_tensor(r2, ds_flat, m2[:], tc2[:].rearrange("p g e -> p (g e)"), ALU.mult, ALU.add)
        nc.scalar.activation(kappa[:], s2[:], ACT.Identity, scale=m3c2[:], bias=b_sum[:])
        nc.vector.scalar_tensor_tensor(term_d, ds_flat.unsqueeze(1).to_broadcast([P, PACK, P]), ac[:], wt,
                                       ALU.subtract, ALU.mult)
        turn_term(term_d, False, False)
        nc.vector.scalar_tensor_tensor(term_f, r2.unsqueeze(1).to_broadcast([P, PACK, P]), kappa[:], w,
                                       ALU.add, ALU.mult)
        turn_term(term_f, False, True)
        gt_planes = sb.tile([P, PACK, Q], BF16, name="gt_planes")
        for t in range(PACK):
            nc.scalar.activation(gt_planes[:, t, :], gt_ps[t][:, 0:Q], ACT.Copy, scale=fs_sb[:, t:t + 1])
        interleave(gt_bf, gt_planes[:])
        gather_rows(2)
        gather_rows(3)
        early_codes = sb.tile([P, early + Q], U32, name="early_codes", tag="row_pool3", align_bytes=64)
        early_scales = sb.tile([P, early + Q], U8, name="early_scales", align_bytes=64)
        last_codes = sb.tile([P, P], U32, name="last_codes", align_bytes=64)
        last_scales = sb.tile([P, P], U8, name="last_scales", align_bytes=64)
        nc.vector.quantize_mx(out=early_codes[:].bitcast(FP8X4), scales=early_scales[:],
                              in_=early_bf[:].rearrange("p d t -> p (d t)"))
        nc.vector.quantize_mx(out=last_codes[:].bitcast(FP8X4), scales=last_scales[:],
                              in_=last_bf[:].rearrange("p d t -> p (d t)"))

        out_early = bank("out_early", "bank_d")
        out_last = bank("out_last", "bank_e")
        out_sb = sb.tile([P, D], F32, name="out_sb")
        gt_cols = slice(early, early + Q)
        for dst, codes, scales in ((out_early[:, 0:2 * P], early_codes[:, 0:2 * P], early_scales[:, 0:2 * P]),
                                   (out_early[:, 2 * P:early], early_codes[:, 2 * P:early], early_scales[:, 2 * P:early]),
                                   (out_last[:, 0:P], last_codes[:], last_scales[:])):
            nc.tensor.matmul_mx(out=dst, lhsT=early_codes[:, gt_cols].bitcast(FP8X4), lhsT_scale=early_scales[:, gt_cols],
                                rhs=codes.bitcast(FP8X4), rhs_scale=scales, start=True, stop=True)
        nc.vector.tensor_tensor(out_sb[:, 0:early], out_early[:, 0:early], res_sb[:, 0:early], ALU.add)
        nc.sync.dma_start(out[:, 0:early], out_sb[:, 0:early])
        nc.vector.tensor_tensor(out_sb[:, early:D], out_last[:, 0:P], res_sb[:, early:D], ALU.add)
        nc.sync.dma_start(out[:, early:D], out_sb[:, early:D])
